import numpy as np, ml_dtypes
CORES = [8,9,10,11,12,13]
N = 6
BF = ml_dtypes.bfloat16
def gentries(a):
    return np.ascontiguousarray(a.reshape(8, 16, -1).transpose(0, 2, 1)).reshape(8, -1)
def gtable(e):
    e = np.asarray(e); return np.ascontiguousarray(e.reshape(8, -1, 16).transpose(0, 2, 1)).reshape(128, -1).astype(np.int32)
VA, G, OB, W, CAP, S = 1024, 512, 2560, 4096, 256, 272
E0, M, RO = 3, 13, 5
WA, NIL = VA + G, W - 1
H = NIL - OB
KC = 6
def within(rng, ke, k):
    o = np.argsort(ke, kind="stable"); cnt = np.bincount(ke, minlength=KC); lo = np.add.accumulate(cnt) - cnt
    i = lo[k] + (rng.random(k.shape) * np.maximum(cnt[k], 1)).astype(np.int64)
    return o[np.minimum(i, ke.size - 1)]
def feat(rng, cen, k, a):
    v = np.swapaxes(cen[np.arange(8)[None, :, None], k], 2, 3)
    return v + rng.integers(-a, a + 1, v.shape)
def parts(rng, bd=None):
    if bd is None: bd = np.argsort(rng.random((N, 8, VA)), axis=-1)[..., :G]
    cen = rng.integers(-90, 91, (8, KC, 16)); ka = rng.integers(0, KC, (N, 8, VA)); kb = rng.integers(0, KC, (N, 8, OB))
    kx = np.concatenate([ka, np.take_along_axis(np.roll(ka, 1, axis=0), np.roll(bd, 1, axis=0), 2)], axis=2)
    eo = np.argsort(kx[:, :, None, :] + 1.5 * rng.random((N, 8, 16, WA)), axis=-1); ao = np.argsort(ka[:, :, None, :] + 1.5 * rng.random((N, 8, 16, VA)), axis=-1)
    nba = np.empty((N, 8, 16, VA), np.int64); np.put_along_axis(nba, ao, eo[..., np.arange(VA) * WA // VA], -1)
    ky = np.concatenate([kb, np.roll(kb, -1, axis=0)[..., :H]], axis=2); nbb = np.empty((N, 8, 16, OB), np.int64); f0 = np.empty((N, 8, 16, S), np.int64)
    dens = rng.choice(np.array([0.3, 0.5, 0.8]), (N, 8))
    for r in range(N):
        for g in range(8):
            k = np.where(rng.random((16, OB)) < 0.75, kb[r, g], rng.integers(0, KC, (16, OB)))
            nbb[r, g] = np.where(rng.random((16, OB)) < 0.04, NIL, within(rng, ky[r, g], k))
            keep = (rng.random((16, S)) < dens[r, g]) & (rng.random((1, S)) > 0.1)
            f0[r, g] = np.where(keep, within(rng, ky[r, g], np.broadcast_to(ka[r, g, :S], (16, S))), NIL)
    return dict(cen=cen, ka=ka, kb=kb, bd=bd, nba=nba, nbb=nbb, f0=f0, xa=feat(rng, cen, ka, 3), xb=feat(rng, cen, kb, 3))
def pack(d):
    t = lambda v, w: np.ascontiguousarray(np.reshape(v, (N, 128, w)))
    return {"xa": t(d["xa"], VA).astype(np.float32).astype(BF), "xb": t(d["xb"], OB).astype(np.float32).astype(BF), "nba": t(d["nba"], VA).astype(np.int32),
            "nbb": t(d["nbb"], OB).astype(np.int32), "f0": t(d["f0"], S).astype(np.int32), "bd": np.stack([gtable(a) for a in d["bd"]])}
def put(row, c, v):
    o = np.setdiff1d(np.arange(row.size), c); hit = o[np.isin(row[o], v)]
    row[hit] = np.setdiff1d(row[c], v)[:hit.size]; row[c] = v
def short(rng, d, r, g):
    z1, z2, x = S, S + 1, VA - 1; P = np.array([S // 4, S // 2, 3 * S // 4, VA - 4, VA - 3, VA - 2])
    T = rng.permutation(np.setdiff1d(np.arange(S), P[:3])); D1, D2 = int(T[0]), int(T[1]); T = T[2:]
    f = d["f0"][r, g]; f[:] = rng.integers(0, NIL, f.shape); f[:, P[:3]] = NIL; f[:15, D1] = NIL; f[:15, D2] = NIL
    m = np.concatenate([P[:3], np.arange(S + 2, VA)])
    for p in range(16):
        c, v = [z1, z2], [D1, D2]
        if p == 0: c, v = [z1, z2, x], [x, z1, int(T[0])]
        elif p == 1: v = [z2, D2]
        elif p == 2: c, v = [z1, z2, x], [D1, D2, z1]
        elif p < 9: c, v = [z1, z2, int(P[p - 3])], [D1, D2, z2]
        elif p < 15:
            i = m[(p - 9) * T.size:(p - 8) * T.size]; c, v = np.concatenate([c, i]), np.concatenate([v, T[:i.size]])
        else: v = [z1, z2]
        put(d["nba"][r, g, p], np.array(c, np.int64), np.array(v, np.int64))
def lone(rng, d, r, g, z0, L):
    c, u, w = OB - 1, VA - 1, S
    f = d["f0"][r, g]; nb = d["nba"][r, g]; v = rng.integers(0, NIL - 1, S)
    f[:] = NIL; f[rng.integers(0, 16, S), np.arange(S)] = v + (v >= c); f[:, 64 + rng.permutation(S - 64)[:z0]] = NIL
    f[:, 0] = NIL; f[0, 0] = NIL - 1; f[1:3, 1] = c
    cells = [0, u, w] if L == 0 else [u, u - 1] + [S + i for i in range(L)]
    d["xa"][r, g][:, cells] = 40; d["xb"][r, g][:, c] = 40; d["nbb"][r, g][:, c] = c
    for p in range(16):
        if L == 0:
            to = {u: p}
            if p == 1: to[w] = u
            if p == 2: to[0] = 1
            if p == 3: to[0] = w
        else:
            to = {u: 1 if p == 1 else S, u - 1: S if p == 1 else (1 if p == 2 else p)}
            for i in range(1, L + 1): to[S + i - 1] = u if p == 4 + i else (S + i if p == 3 and i < L else 16 * i + p)
        k = sorted(to); put(nb[p], np.array(k, np.int64), np.array([to[i] for i in k], np.int64))
def quiet(rng, d, r):
    for g in range(8):
        o = rng.permutation(min(S, CAP)); x, y = int(o[0]), int(o[1]); z = int(rng.integers(2 * CAP + 1, VA)); c = int(rng.integers(0, OB))
        d["f0"][r, g] = NIL; d["f0"][r, g][:, y] = c
        for p in range(16):
            d["nba"][r, g, p] = rng.permutation(VA)
            if p == 0: k, v = [x, y], [y, x]
            else: k, v = [x, z, y], [x, y, z]
            put(d["nba"][r, g, p], np.array(k, np.int64), np.array(v, np.int64))
        b = d["xb"][r, g][:, c]; d["xa"][r, g][:, x] = b + (E0 if g < 7 else E0 + 1); d["xa"][r, g][:, z] = b - (E0 + 1)
def setup_inputs(rng):
    return pack(parts(rng))
def setup_inputs_room(rng):
    d = parts(rng); d["xa"] = feat(rng, d["cen"], d["ka"], 1); d["xb"] = feat(rng, d["cen"], d["kb"], 1); z0 = (S - VA) % CAP
    d["xa"][:, ::2, M - 1:] = 127; d["xb"][:, ::2, M - 1:] = -127; d["xa"][:, 1::2, M:] = 127; d["xb"][:, 1::2, M:] = -127
    d["xa"][:, 1::4, :M] = rng.integers(-1, 2, (N, 2, M, VA)); d["xb"][:, 1::4, :M] = rng.integers(-1, 2, (N, 2, M, OB))
    for r in range(N):
        for g in (0, 4):
            z = z0 + (0, 1, -1)[(r + g // 2) % 3]; o = rng.permutation(S)
            d["f0"][r, g][:, o[:z]] = NIL; d["f0"][r, g, rng.integers(0, 16, S - z), o[z:]] = rng.integers(0, NIL, S - z)
        lone(rng, d, r, 2, z0, 0); lone(rng, d, r, 6, z0, RO - (VA - S + z0) // CAP)
        for g in (1, 5): short(rng, d, r, g)
    return pack(d)
def setup_inputs_ties(rng):
    d = parts(rng); d["xb"] = feat(rng, d["cen"], d["kb"], 0); v = feat(rng, d["cen"], d["ka"], 0)
    d["xa"] = v + rng.choice(np.array([0, E0, E0 + 1, E0 + 2]), v.shape, p=[0.3, 0.55, 0.12, 0.03]) * rng.choice(np.array([-1, 1]), v.shape)
    d["f0"][:, ::2] = d["f0"][:, ::2, :1].copy(); d["nbb"][:, 1::2] = d["nbb"][:, 1::2, 5:6].copy(); d["nbb"][:, 0, 15] = np.arange(OB)
    quiet(rng, d, 0)
    return pack(d)
def setup_inputs_ends(rng):
    o = 1 + np.argsort(rng.random((N, 8, VA - 2)), axis=-1)[..., :G - 2]; z = np.zeros((N, 8, 1), np.int64)
    d = parts(rng, np.concatenate([z, o, z + VA - 1], axis=2)); ends = np.array([0, H - 1, H, OB - 1, OB, W - 2, NIL])
    d["cen"][::2] = d["cen"][::2, :1].copy(); d["cen"][4] = 125; d["cen"][6] = -125
    d["xa"] = feat(rng, d["cen"], d["ka"], 2); d["xb"] = feat(rng, d["cen"], d["kb"], 2)
    d["f0"] = np.where(rng.random(d["f0"].shape) < 0.5, rng.choice(ends, d["f0"].shape), d["f0"])
    e = d["nbb"][:, ::2]; d["nbb"][:, ::2] = np.where(rng.random(e.shape) < 0.5, rng.choice(ends, e.shape), e)
    d["nbb"][:, 5] = NIL; d["f0"][0, 7] = NIL; d["nba"][:, 2, 0] = np.arange(VA); d["nba"][:, 2, 1] = WA - 1 - np.arange(VA)
    return pack(d)
def setup_inputs_cross(rng):
    h = min(S, G) // 2; a = np.argsort(rng.random((N, 8, S)), axis=-1)[..., :h]; b = S + np.argsort(rng.random((N, 8, VA - S)), axis=-1)[..., :G - h]
    bd = np.concatenate([a, b], axis=2); bd = np.take_along_axis(bd, np.argsort(rng.random(bd.shape), axis=-1), 2); d = parts(rng, bd)
    noise = np.full((1, 8, 1, 1), 3); noise[:, :2] = 1; d["xa"] = feat(rng, d["cen"], d["ka"], noise); d["xb"] = feat(rng, d["cen"], d["kb"], noise)
    for r in range(N):
        for g in range(8):
            far = OB + within(rng, d["kb"][(r + 1) % N, g, :H], np.broadcast_to(d["ka"][r, g, :S], (16, S))); f = d["f0"][r, g]
            d["f0"][r, g] = np.where((f != NIL) & (rng.random(f.shape) < 0.8), far, f)
    d["f0"][1::2, :4] = NIL; lo = np.arange(VA) < CAP
    for r in range(1, N, 2):
        for g in (0, 1):
            for p in range(16):
                row = d["nba"][r, g, p]; gh = row >= VA
                i = np.flatnonzero(gh & (lo == (g == 0))); j = np.flatnonzero(~gh & (lo == (g == 1))); k = min(i.size, j.size); i = i[:k]; j = j[:k]
                vi = row[i].copy(); row[i] = row[j]; row[j] = vi
    return pack(d)
def setup_inputs_spread(rng):
    d = parts(rng); cen = rng.integers(-127, 128, (8, KC, 16))
    for x, k, n in (("xa", d["ka"], VA), ("xb", d["kb"], OB)):
        v = np.clip(feat(rng, cen, k, rng.choice(np.array([0, 1, 2, 2, 3, 3, 5, 12]), (N, 8, 1, n))), -127, 127)
        v = np.where(rng.random((N, 8, 1, n)) < 0.125, rng.integers(-127, 128, v.shape), v)
        d[x] = v * (rng.random((N, 8, 1, n)) > 0.0625)
    d["nba"][:, :, 4:8] = np.argsort(rng.random((N, 8, 4, WA)), axis=-1)[..., :VA]
    d["nbb"] = np.where(rng.random(d["nbb"].shape) < 0.3, rng.integers(0, W, d["nbb"].shape), d["nbb"])
    return pack(d)
def check_inputs(d):
    bad = []
    for k, hi in (("nba", WA - 1), ("nbb", NIL), ("f0", NIL), ("bd", VA - 1)):
        if np.min(d[k]) < 0 or np.max(d[k]) > hi: bad.append("range of " + k)
    for k in ("xa", "xb"):
        v = d[k].astype(np.float32)
        if not np.all((v >= -127) & (v <= 127) & (np.rint(v) == v)): bad.append("whole numbers of " + k)
    s = np.sort(d["nba"], axis=2)
    if np.any(s[..., 1:] == s[..., :-1]): bad.append("repeated in a row of nba")
    s = np.sort(np.stack([gentries(a) for a in d["bd"]]), axis=2)
    if np.any(s[..., 1:] == s[..., :-1]): bad.append("repeated in bd")
    return bad
def reference(xa, xb, nba, nbb, f0, bd):
    A = xa.astype(np.float32).astype(np.int32).reshape(N, 8, 16, VA); own = xb.astype(np.float32).astype(np.int32).reshape(N, 8, 16, OB)
    na = nba.astype(np.int64).reshape(N, 8, 16, VA); no = nbb.astype(np.int64).reshape(N, 8, 16, OB); bl = np.stack([gentries(a) for a in bd]).astype(np.int64)
    B = np.zeros((N, 8, 16, W), np.int32); NB = np.full((N, 8, 16, W), NIL, np.int64)
    for r in range(N):
        q = (r + 1) % N; n = no[q, :, :, :H]
        B[r, :, :, :OB] = own[r]; B[r, :, :, OB:NIL] = own[q, :, :, :H]
        NB[r, :, :, :OB] = no[r]; NB[r, :, :, OB:NIL] = np.where(n < H, OB + n, NIL)
    F = np.full((N, 8, 16, VA), NIL, np.int64); F[..., :S] = f0.reshape(N, 8, 16, S)
    flag = np.ones((N, 8, VA), bool); e = [E0] * N; rows = np.arange(16)[:, None]
    for wave in range(RO):
        ext = []
        for r in range(N):
            q = (r - 1) % N; n = np.take_along_axis(F[q], bl[q][:, None, :], 2)
            ext.append(np.concatenate([F[r], np.where((n >= OB) & (n < NIL), n - OB, NIL)], axis=2))
        for r in range(N):
            good = 0
            for g in range(8):
                a = np.flatnonzero(flag[r, g] & np.all(F[r, g] == NIL, axis=0))[:CAP]
                x = A[r, g][:, a]; c = ext[r][g][rows, na[r, g][:, a]]; col = np.arange(a.size)
                new = np.full(c.shape, NIL, np.int64)
                for t in range(3):
                    near = (np.abs(B[r, g][:, c] - x[:, None, :]) <= e[r]).astype(np.int32)
                    v = (c != NIL) & (np.add.reduce(near, axis=0) >= M); new = np.where(v, c, new); some = np.any(v, axis=0)
                    if t == 0:
                        ok = some; b = np.where(ok, c[np.argmax(v, axis=0), col], NIL)
                    else:
                        b = np.where(some, c[15 - np.argmax(v[::-1], axis=0), col], b)
                    c = NB[r, g][:, b]
                s = a[ok]; b = b[ok]; F[r, g][:, s] = new[:, ok]
                A[r, g][:, s] = x[:, ok] + np.clip(B[r, g][:, b] - x[:, ok], -2, 2)
                flag[r, g, a] = False
                w = na[r, g][:, s].reshape(-1); flag[r, g, w[w < VA]] = True
                good += int(s.size)
            e[r] = E0 + (good & 1)
    return {"yf": F.reshape(N, 128, VA).astype(np.float32), "ya": A.reshape(N, 128, VA).astype(np.float32).astype(BF)}

from concourse.mybir import AluOpType, AxisListType, ActivationFunctionType

OP = AluOpType
AF = ActivationFunctionType
NOWN, NG, NB_, NS0, WAVES, H = 1024, 512, 2560, 34, 5, 1535
DUMP, EW, GB = 1024, 1280, 1280
EALL = GB + NG
C0 = NS0 * 16
MAG = 100663296.0
WT = 32768.0
GC, SC, LOOK = 0.0016, 0.0040, 0.05
REM, WAKE, PEC = 4.0, 0.06, 0.00085
ROUND_S = [(0, 0, 1), (0, 1, 1)]

SIZE = {"float32": 4, "int32": 4, "bfloat16": 2, "float16": 2, "uint16": 2}
SCRATCH = {}
for _d, _l in (
        ("bfloat16", "BT 4112 XA 1280 YA 1280 XR0 4096 XR1 4096 FLB 1024 FMB 1024 DGB 2048 NX 256 BG 1024 IB 128 INB 128"),
        ("int32", "NBT 4104 NBX 1536 NAT 1280 NTMP 1024 F0 272 FI 272 FA 272 BD 32 IO 16 IO2 16 PI 1 PU 1 PQ 1 PV 1 FIN 256 FIA 256 "
                  "BC 16 BI 16 PINT 1"),
        ("uint16", "BDU 32 OFU 64 IDR 256 IXU 16 NAU 256 CU 256 BU 16 MO 256 ISU 16"),
        ("float16", "SG 4096 DD_ 4096 NR 4096 DUMPR 256 ISN 272 BO 128 BON 128 BOB 128 I16 128 TRI 128 QF 128 QL 128 O16 128 SV 512 DG 2048 "
                    "Z0 144 Z1 144 Z2 144 Z3 144 AV 64 IDF 256 V 256 SEL 256 SELC 256 OFFS 256 OT 256 PR16 1 DX 256 CL 256"),
        ("float32", "E 1792 YF 1280 YT 1024 FL 1792 FM 1792 IDXW 2048 CELLV 1024 DEF 256 CA 64 MV 1280 GS 512 ONES 128 BOA 128 BOF 128 IF 128 "
                    "UPF 128 S1F 128 S2F 128 TF 128 MK 16 PUF 1 PM 1 PN 1 IS 64 MC 8 NE 64 NT 64 T2 64 T3 64 XX 64 WTL 64 CS 65 U1 64 OF 64 "
                    "INF 64 IXF 16 PH 256 CS0 256 FN 256 CS2 256 ACC 256 M 256 Y 256 B0 16 TS 16 TS2 16 PC 16 PR 1 NAF 256")):
    _l = _l.split()
    for _i in range(0, len(_l), 2):
        SCRATCH[_l[_i]] = ("sbuf", [128, int(_l[_i + 1])], _d)
PSUM = ("A0", "A1", "B0P", "B1P", "MP", "M5", "F6", "F7")
for _n in PSUM:
    SCRATCH[_n] = ("psum", [128, 512], "float32")

LOADS = ("f0", "bd", "naA", "xaA", "xb", "nbA", "nbB", "naB", "xaB", "yaL", "oF", "oA")
SEMAPHORES = (["cV", "cS", "cP", "cG", "bArr", "nArr", "bLoc", "nLoc", "crLoc"] + ["d_" + x for x in LOADS]
              + ["gArr%d" % w for w in range(WAVES)] + ["gLoc%d" % w for w in range(WAVES)] + ["cred%d" % w for w in range(1, WAVES)])


def rank_program(g, core, T, topo):
    rank = T.rank_of(core)
    if rank is None:
        return
    n = len(T.cores)
    nxt, prv = T.cores[(rank + 1) % n], T.cores[(rank - 1) % n]
    Q = {"V": g.vector, "S": g.scalar, "P": g.tensor, "G": g, "Y": g.sync}
    cnt = {q: 0 for q in "VSPG"}
    seen = {q: {} for q in Q}
    know = {}
    wr, rd = {}, {}
    ops = []
    loads = {}

    def need(q, tok):
        s, v = tok
        if seen[q].get(s, 0) >= v:
            return
        Q[q].wait_ge(T.sem[s], v)
        seen[q][s] = v
        for s2, v2 in know.get(tok, {}).items():
            if seen[q].get(s2, 0) < v2:
                seen[q][s2] = v2

    def conflicts(q, reads, writes, wr, rd, same_order):
        out = []
        for (nm, lo, hi) in reads:
            ps = nm in PSUM
            out += [(e[3], True) for e in wr.get(nm, ()) if ps or (e[0] < hi and lo < e[1])]
            if ps:
                out += [(e[3], e[2] != q) for e in rd.get(nm, ()) if same_order or e[2] != q]
        for (nm, lo, hi) in writes:
            ps = nm in PSUM
            out += [(e[3], e[2] != q or not ps) for e in wr.get(nm, []) + rd.get(nm, [])
                    if (ps or (e[0] < hi and lo < e[1])) and (same_order or e[2] != q or not ps)]
        return out

    def note(q, reads, writes, tok, wr, rd):
        for (nm, lo, hi) in writes:
            if nm in PSUM:
                lo, hi = 0, 512
            wr[nm] = [e for e in wr.get(nm, ()) if not (lo <= e[0] and e[1] <= hi)] + [(lo, hi, q, tok)]
            rd[nm] = [e for e in rd.get(nm, ()) if not (lo <= e[0] and e[1] <= hi)]
        for (nm, lo, hi) in reads:
            if nm in PSUM:
                lo, hi = 0, 512
            rd[nm] = [e for e in rd.get(nm, ()) if not (e[2] == q and lo <= e[0] and e[1] <= hi)] + [(lo, hi, q, tok)]

    def op(q, reads, writes, cost, lat, emit, after=()):
        ops.append((q, reads, writes, cost, lat, emit, tuple(after)))
        return len(ops) - 1

    def waits(q, reads, writes, dma=False):
        toks = {}
        for tok, _ in conflicts(q, reads, writes, wr, rd, dma):
            toks[tok[0]] = max(toks.get(tok[0], 0), tok[1])
        for s in sorted(toks):
            need(q, (s, toks[s]))

    def run(q, reads, writes, cost, calls):
        def emit():
            waits(q, reads, writes)
            for call in calls:
                cnt[q] += 1
                tok = ("c" + q, cnt[q])
                know[tok] = dict(seen[q])
                call().then_inc(T.sem["c" + q], 1)
            note(q, reads, writes, tok, wr, rd)
        return op(q, reads, writes, cost, 0.06, emit)

    def issue():
        m = len(ops)
        w2, r2 = {}, {}
        dep, succ = [], [[] for _ in range(m)]
        for i, o in enumerate(ops):
            d = {}
            for j, strong in conflicts(o[0], o[1], o[2], w2, r2, True):
                d[j] = d.get(j, False) or strong
            for j in o[6]:
                d[j] = True
            dep.append(d)
            for j in d:
                succ[j].append(i)
            note(o[0], o[1], o[2], i, w2, r2)
        pri = [0.0] * m
        for i in range(m - 1, -1, -1):
            pri[i] = ops[i][3] + max([pri[j] + (ops[i][4] + WAKE if dep[j][i] else 0.0) for j in succ[i]] + [0.0])
        left = [len(d) for d in dep]
        ready = [0.0] * m
        free, avail = {}, {}
        for i, o in enumerate(ops):
            free.setdefault(o[0], 0.0)
            avail.setdefault(o[0], [])
            if not left[i]:
                avail[o[0]].append(i)
        order = []
        while len(order) < m:
            t, q = min((max(free[q], min(ready[i] for i in a)), q) for q, a in avail.items() if a)
            i = max((i for i in avail[q] if ready[i] <= t + LOOK), key=lambda i: (pri[i], -i))
            t = max(t, ready[i])
            avail[q].remove(i)
            free[q] = t + ops[i][3]
            order.append(i)
            for j in succ[i]:
                ready[j] = max(ready[j], t + ops[i][3] + (ops[i][4] + WAKE if dep[j][i] else 0.0))
                left[j] -= 1
                if not left[j]:
                    avail[ops[j][0]].append(j)
        for i in order:
            ops[i][5]()

    def R(nm, lo, hi, st=1):
        return (T[nm][:, lo:hi:st] if st > 1 else T[nm][:, lo:hi], [(nm, lo, hi)])

    def IND(nm, lo, hi, off, a, b):
        return (T[nm][:, lo:hi].indirect(T[off][:, a:b]), [(nm, lo, hi)], [(off, a, b)])

    def full(nm):
        return R(nm, 0, SCRATCH[nm][1][1])

    def hs(nm, h, k=128):
        return R(nm, k * h, k * h + k)

    def ind(x):
        return len(x) > 2

    def rds(*xs):
        r = []
        for x in xs:
            if isinstance(x, tuple):
                r += x[1] + (x[2] if ind(x) else [])
        return r

    def offs(out):
        return out[2] if ind(out) else []

    def ap(x):
        return x[0] if isinstance(x, tuple) else x

    def two(x):
        return SIZE[SCRATCH[x[1][0][0]][2]] == 2

    def width(x):
        return x[0].shape[1]

    def vcost(out, a, k, m):
        if ind(out):
            return 0.07 + m * SC
        if ind(a):
            return 0.07 + m * GC
        return max(0.064, m * k * 0.001)

    def cp(out, a):
        m = width(a) if not ind(a) else width(out)
        run("V", rds(a) + offs(out), out[1], vcost(out, a, 0.5 if two(out) and two(a) else 1.0, m),
            [lambda: g.vector.tensor_copy(out[0], a[0])])

    def tt(out, a, b, f):
        k = 1.0 if a[1][0][0] in PSUM or b[1][0][0] in PSUM else 2.0
        run("V", rds(a, b) + offs(out), out[1], vcost(out, a, k, width(b)), [lambda: g.vector.tensor_tensor(out[0], a[0], b[0], f)])

    def ts(out, a, s1, op0, s2=None, op1=None):
        c = vcost(out, a, 0.5 if two(out) and two(a) else 1.0, width(out))
        if op1 is None:
            run("V", rds(a, s1), out[1], c, [lambda: g.vector.tensor_scalar(out[0], a[0], ap(s1), None, op0)])
        else:
            run("V", rds(a, s1, s2), out[1], c, [lambda: g.vector.tensor_scalar(out[0], a[0], ap(s1), ap(s2), op0, op1)])

    def ms(out, c):
        return run("V", [], out[1], vcost(out, out, 0.5 if two(out) else 1.0, width(out)), [lambda: g.vector.memset(out[0], c)])

    def act(out, a, func, **kw):
        m = width(out) if ind(a) else width(a)
        run("S", rds(a) + offs(out), out[1], 0.02 + vcost(out, a, 1.0, m), [lambda: g.scalar.activation(out[0], a[0], func, **kw)])

    def mms(*group):
        r, w, c, calls = [], [], 0.0, []
        for (out, lhs, rhs, start, stop) in group:
            r += [x for x in rds(lhs, rhs) if x not in r]
            w += [x for x in out[1] if x not in w]
            c += max(64, width(rhs)) * PEC
            calls.append(lambda out=out, lhs=lhs, rhs=rhs, start=start, stop=stop: g.tensor.matmul(out[0], lhs[0], rhs[0], start, stop))
        run("P", r, w, c, calls)

    def aff(out, a, pattern, cmp, base, cm):
        run("G", a[1], out[1], 0.4, [lambda: g.affine_select(out[0], a[0], pattern, cmp, 0.0, base, cm)])

    def iota(out, pattern, base, cm):
        kw = {} if SCRATCH[out[1][0][0]][2] == "int32" else {"allow_small_or_imprecise_dtypes": True}
        run("G", [], out[1], 0.13 + 0.002 * width(out), [lambda: g.iota(out[0], pattern, base, cm, **kw)])

    def load(q, sem, out, in_ap, after=(), fills=()):
        nm, lo, hi = out[1][0]

        def emit():
            for k in after:
                need(q, ("d_" + k, 16))
            if fills:
                waits(q, [], [(nm, 0, hi)], True)
            tok = ("d_" + sem, 16)
            know[tok] = dict(seen[q])
            Q[q].dma_start(out[0], in_ap).then_inc(T.sem["d_" + sem], 16)
            note("dma", [], out[1], tok, wr, rd)
        loads[sem] = op(q, [], out[1], 0.1, 2.0 + (hi - lo) * SIZE[SCRATCH[nm][2]] * 128 / 150e3, emit, [loads[k] for k in after] + list(fills))

    def store(q, sem, out_ap, a):
        def emit():
            waits(q, a[1], [], True)
            Q[q].dma_start(out_ap, a[0]).then_inc(T.sem["d_" + sem], 16)
        op(q, a[1], [], 0.1, 3.0, emit)

    def send(dst, src, out, a, rsem, lsem, cred=None):
        ne = len(topo.engines(core, dst))
        ad = topo.addr(dst)

        def emit():
            waits("G", a[1], [])
            if cred:
                need("G", (cred, 1))
            g.remote_dma(out_ap=out[0], in_ap=a[0], remote_sem=T.sem[rsem], local_sem=T.sem[lsem], pid=ad[1], routing_id=ad[0],
                         dma_engine_mask=topo.mask(core, dst))
            tok = (lsem, ne)
            know[tok] = dict(seen["G"])
            note("snd", a[1], [], tok, wr, rd)
        i = op("G", a[1], [], 0.5, REM, emit)
        op("R", [], out[1], 0.0, 0.0, lambda: note("rem", [], out[1], (rsem, len(topo.engines(src, core))), wr, rd), [i])

    def credit(w):
        ad = topo.addr(prv)

        def emit():
            waits("G", [], [("E", GB, EALL)])
            g.remote_sem_update(T.sem["cred%d" % w], T.sem["crLoc"], ad[1], ad[0], 1 << topo.engines(core, prv)[0])
        op("G", [], [("E", GB, EALL)], 0.3, 2.0, emit)

    fb, fn = ms(R("BT", 0, 16), 512.0), ms(R("NBT", 0, 8), 4095)
    load("Y", "f0", full("F0"), T.f0[:])
    load("S", "bd", full("BD"), T.bd[:])
    load("S", "xaA", R("XA", 0, C0), T.xa[:, 0:C0])
    load("Y", "naA", R("NAT", 0, C0), T.nba[:, 0:C0])
    load("Y", "xb", R("BT", 1, 1 + NB_), T.xb[:], (), [fb])
    load("Y", "nbA", R("NBT", 1, 1 + H), T.nbb[:, 0:H], (), [fn])
    load("Y", "nbB", R("NBT", 1 + H, 1 + NB_), T.nbb[:, H:NB_], ["xb"], [fn])
    load("Y", "naB", R("NAT", C0, NOWN), T.nba[:, C0:NOWN])
    load("Y", "xaB", R("XA", C0, NOWN), T.xa[:, C0:NOWN])
    load("Y", "yaL", R("YA", 0, NOWN), T.xa[:])

    def ghosts(w):
        ts(full("GS"), IND("E", 0, NOWN, "BDU", 0, 32), -2560.0, OP.add, 0.0, OP.max)
        send(nxt, prv, R("E", GB, EALL), full("GS"), "gArr%d" % w, "gLoc%d" % w, "cred%d" % w if w else None)

    ms(full("ONES"), 1.0)
    ms(R("E", 272, EW), 0.0)
    ts(full("FI"), full("F0"), 1, OP.add)
    ts(full("FA"), full("FI"), 4095, OP.bitwise_and)
    cp(R("E", 0, 272), full("FA"))
    cp(full("BDU"), full("BD"))
    ts(full("ISN"), full("F0"), 4095, OP.is_equal)
    ghosts(0)
    send(prv, nxt, R("BT", 2561, 4096), R("BT", 1, 1 + H), "bArr", "bLoc")
    iota(full("IO"), [[-1, 16]], 16, 1)
    iota(full("PI"), [[0, 1]], 0, 1)
    aff(full("BOA"), full("ONES"), [[-16, 8], [0, 16]], OP.is_ge, 0, 1)
    aff(full("BOF"), full("BOA"), [[16, 8], [0, 16]], OP.is_ge, 15, -1)
    aff(full("IF"), full("ONES"), [[-1, 128]], OP.is_equal, 0, 1)
    aff(full("UPF"), full("BOF"), [[1, 128]], OP.is_gt, 0, -1)
    iota(full("IS"), [[16, 64]], DUMP, 0)
    iota(full("CELLV"), [[1, 1024]], 64, 0)
    iota(full("DEF"), [[1, 256]], DUMP + 64, 0)
    aff(full("S1F"), full("ONES"), [[1, 128]], OP.is_equal, -16, -1)
    aff(full("S2F"), full("ONES"), [[1, 128]], OP.is_equal, 16, -1)
    ts(full("IO2"), full("IO"), 15, OP.bitwise_and)
    ts(full("PU"), full("PI"), 15, OP.bitwise_and)
    ts(full("PQ"), full("PI"), 4, OP.logical_shift_right)
    cp(full("PUF"), full("PU"))
    ts(full("MK"), full("IO2"), 0, OP.is_equal)
    ts(full("PV"), full("PQ"), 1, OP.bitwise_and)
    cp(full("PM"), full("PV"))
    ts(full("PN"), full("PM"), -1.0, OP.mult, 1.0, OP.add)
    bo8 = (T["BOF"][:, 0:128:16], [("BOF", 0, 128)])
    for z, v in (("Z1", 1.0), ("Z0", WT), ("Z2", 2048.0), ("Z3", 6144.0)):
        ms(full(z), 0.0)
        ts((T[z][:, 15:143:16], [(z, 0, 144)]), bo8, v, OP.mult)

    def sel(z, p):
        return R(z, 15 - p, 143 - p)

    mms(*[(R("F7", 0, 17), sel("Z1", c), R("ISN", c, 272, 16), c == 0, c == 15) for c in range(16)])
    cp(full("BO"), full("BOF"))
    ts(full("TF"), full("IF"), -2047.0, OP.mult)
    tt(full("TRI"), full("TF"), full("UPF"), OP.add)
    ms(R("CS", 0, 1), 2047.0)
    ts(full("CA"), full("IS"), full("PUF"), OP.add)
    ms(full("AV"), 1.0)
    ms(full("NE"), 0.0)
    ms(full("WTL"), 1.0)
    ts(R("AV", 0, 17), R("F7", 0, 17), 15.5, OP.is_gt)
    ts(R("NE", 0, 17), R("F7", 0, 17), 15.5, OP.is_lt)

    def front_a(w, ns):
        mms((R("F6", 0, ns), full("TRI"), R("AV", 0, ns), True, True))
        mms((R("F6", 64, 64 + ns), full("BO"), R("AV", 0, ns), True, True))
        run("V", rds(R("ONES", 0, ns), R("F6", 64, 64 + ns)), [("CS", 1, 1 + ns)], 0.07,
            [lambda: g.vector.tensor_tensor_scan(T["CS"][:, 1:1 + ns], T["ONES"][:, 0:ns], T["F6"][:, 64:64 + ns], 2047.0, OP.mult, OP.add)])
        tt(R("U1", 0, ns), R("F6", 0, ns), R("CS", 0, ns), OP.add)
        tt(R("OF", 0, ns), R("U1", 0, ns), R("CA", 0, ns), OP.min)
        cp(R("OFU", 0, ns), R("OF", 0, ns))
        act(R("IDXW", 0, 256), full("DEF"), AF.Copy)
        act(IND("IDXW", 0, 2048, "OFU", 0, ns), R("CELLV", 0, 16 * ns), AF.Silu)
        ts(R("INF", 0, ns), R("U1", 0, ns), 256.0, OP.is_lt)
        tt(R("WTL", 0, ns), R("AV", 0, ns), R("INF", 0, ns), OP.subtract)

    def front_b(w):
        hi = C0 if w == 0 else EW
        ts(full("IDF"), R("IDXW", 0, 256), -64.0, OP.add)
        ts(full("IDR"), R("IDXW", 0, 256), -63.75, OP.add)
        mms(*[(R("F7", 0, 16), R("DG", c * 128, c * 128 + 128), R("IDF", c, 256, 16), c == 0, c == 15) for c in range(16)])
        for k in range(4):
            act(R("XR%d" % (w % 2), 1024 * k, 1024 * k + 1024), IND("XA", 0, hi, "IDR", 64 * k, 64 * k + 64), AF.Identity)
        ts(full("IXU"), R("F7", 0, 16), 0.25, OP.add)
        cp(full("NAU"), IND("NAT", 0, hi, "IXU", 0, 16))
        cp(full("IXF"), full("IXU"))
        cp(full("NAF"), full("NAU"))

    def remap(lo, hi):
        ts(R("NTMP", lo, hi), R("NAT", lo, hi), 1024, OP.is_ge, 256, OP.mult)
        tt(R("NAT", lo, hi), R("NAT", lo, hi), R("NTMP", lo, hi), OP.add)

    front_a(0, NS0)
    for c in range(16):
        ts(R("DG", c * 128, c * 128 + 128), full("IF"), R("MK", c, c + 1), OP.mult)
    remap(0, C0)
    front_b(0)
    ms(full("MC"), MAG + 8.0)
    ms(R("BT", 4096, 4112), 512.0)
    ms(R("NBT", 4096, 4104), 4095)
    ts(full("BOB"), full("BOF"), -12.5 * WT / 16, OP.mult)
    ms(full("O16"), 1.0)
    tt(full("QF"), full("UPF"), full("IF"), OP.subtract)
    tt(full("TF"), full("BOF"), full("UPF"), OP.subtract)
    tt(full("TF"), full("TF"), full("IF"), OP.subtract)
    tt(full("QL"), full("TF"), full("IF"), OP.subtract)
    ts(R("NBX", 0, H), R("NBT", 1, 1 + H), 1535, OP.min, 2560, OP.add)
    send(prv, nxt, R("NBT", 2561, 4096), R("NBX", 0, H), "nArr", "nLoc")
    ts(full("BON"), full("BOF"), -4096.0, OP.mult)
    cp(full("I16"), full("IF"))
    ts(full("DUMPR"), full("DEF"), -64.0, OP.add)
    ts(R("SV", 0, 128), full("IF"), full("PN"), OP.mult)
    ts(R("SV", 128, 256), full("S1F"), full("PN"), OP.mult)
    ts(R("SV", 256, 384), full("S2F"), full("PM"), OP.mult)
    ts(R("SV", 384, 512), full("IF"), full("PM"), OP.mult)
    cp(full("DGB"), full("DG"))
    cp(full("IB"), full("IF"))
    ts(full("INB"), full("IF"), -1.0, OP.mult)
    for w in range(4):
        ms(R("MV", 256 * w, 256 * w + 256), 4.0 * w + 4.0)
    ms(R("MV", 1024, 1280), 100.0)
    ms(full("FL"), 0.0)
    ms(full("FM"), 0.0)
    ms(R("NAT", NOWN, EW), DUMP)
    ms(R("XA", NOWN, EW), 0.0)
    ms(R("YA", NOWN, EW), 0.0)
    remap(C0, NOWN)

    def A(h):
        return "A%d" % h

    def B(h):
        return "B%dP" % h

    def seeds(h, q):
        o = h * 128 + q * 64
        out = R(A(h), 64 * q, 64 * q + 64)
        ts(R("SG", o * 16, o * 16 + 1024), IND("E", 0, EALL, "NAU", o, o + 64), -2048.0, OP.add)
        mms(*[(out, R("DG", p * 128, p * 128 + 128), R("SG", o * 16 + p, o * 16 + 1024, 16), p == 0, p == 15) for p in range(16)])

    def seeds_end(h):
        ts(hs("CU", h), R(A(h), 0, 128), 2048.0, OP.add)
        act(hs("PH", h), R(A(h), 0, 128), AF.Identity)
        act(hs("CS0", h), R(A(h), 0, 128), AF.Identity, bias=-4096.0)

    def near(w, t, h, q):
        o = h * 128 + q * 64
        m = R("MC", w, w + 1)
        xr = "XR%d" % (w % 2)
        if (t, h, q) in ROUND_S:
            act(full("BG"), IND("BT", 0, 4097, "CU", o, o + 64), AF.Identity)
            for k, bank in enumerate(("M5", "F6")):
                c = o * 16 + 512 * k
                mms((R(bank, 0, 512), full("IB"), R("BG", 512 * k, 512 * k + 512), True, False),
                    (R(bank, 0, 512), full("INB"), R(xr, c, c + 512), False, True))
                ts(R("NR", c, c + 512), R(bank, 0, 512), m, OP.add, m, OP.is_equal)
        else:
            tt(R("DD_", o * 16, o * 16 + 1024), IND("BT", 0, 4097, "CU", o, o + 64), R(xr, o * 16, o * 16 + 1024), OP.subtract)
            ts(R("NR", o * 16, o * 16 + 1024), R("DD_", o * 16, o * 16 + 1024), m, OP.add, m, OP.is_equal)
        out = R(A(h), 64 * q, 64 * q + 64)
        mms((out, full("BOB"), R("O16", 0, 64), True, False),
            *[(out, sel("Z0", p), R("NR", o * 16 + p, o * 16 + 1024, 16), False, p == 15) for p in range(16)])

    def seg1(w, t, h):
        a = R(A(h), 0, 128)
        ts(hs("V", h), a, 0.0, OP.is_gt)
        mms((R(B(h), 0, 128), full("QF" if t == 0 else "QL"), hs("V", h), True, True))
        if t == 0:
            tt(hs("ACC", h), a, hs("CS0", h), OP.min)
        elif t == 1:
            tt(hs("M", h), a, hs("FN", h), OP.min)
            tt(hs("ACC", h), hs("ACC", h), hs("M", h), OP.max)
        else:
            tt(hs("M", h), a, hs("CS2", h), OP.min)
            tt(hs("FIN", h), hs("Y", h), hs("M", h), OP.max)
            ts(hs("FIA", h), hs("FIN", h), 4095, OP.bitwise_and)
            cp(IND("YF" if w == WAVES - 1 else "E", 0, EW, "IXU", 8 * h, 8 * h + 8), hs("FIA", h))

    def seg2(w, t, h):
        ts(hs("SEL", h), R(B(h), 0, 128), 0.0, OP.is_lt)
        tt(hs("SELC", h), hs("SEL", h), hs("PH" if t == 0 else "FN", h), OP.mult)
        out = R(B(h), 128, 136)
        z = "Z2" if t == 0 else "Z3"
        mms(*[(out, sel(z, c), R("SEL", 128 * h + c, 128 * h + 128, 16), c == 0, False) for c in range(16)],
            *[(out, sel("Z1", c), R("SELC", 128 * h + c, 128 * h + 128, 16), False, c == 15) for c in range(16)])

    def seg3(w, t, h):
        x = R(B(h), 128, 136)
        b = hs("BU", h, 8)
        if t == 0:
            cp(b, x)
            cp(hs("B0", h, 8), x)
        else:
            tt(hs("BC", h, 8), x, hs("B0" if t == 1 else "BI", h, 8), OP.max)
            ts(hs("BI", h, 8), hs("BC", h, 8), 4095, OP.bitwise_and)
            cp(b, hs("BI", h, 8))
        if t < 2:
            ts(hs("FN", h), IND("NBT", 0, 4097, "BU", 8 * h, 8 * h + 8), -2047.0, OP.add)
            ts(hs("CU", h), hs("FN", h), 2048.0, OP.add)
        if t == 1:
            last = w == WAVES - 1
            ts(hs("CS2", h), hs("FN", h), 10240.0 - (1.0 if last else 0.0), OP.add)
            ts(hs("Y", h), hs("ACC", h), 6144.0, OP.add, 0.0, OP.max)
            if last:
                ts(hs("Y", h), hs("Y", h), -1.0, OP.add)

    def idxs(w):
        ts(full("TS"), full("B0"), 0.0, OP.is_equal, 4096.0, OP.mult)
        tt(full("TS"), full("TS"), R("CA", 0, 16), OP.min)
        tt(full("TS2"), full("TS"), full("IXF"), OP.max)
        cp(full("ISU"), full("TS2"))

    def marks(w, h):
        o = R("MP", 128 * h, 128 * h + 128)
        mms((o, full("BON"), hs("SEL", h), True, False), (o, full("I16"), hs("DUMPR", h), False, True))
        tt(hs("OFFS", h), o, hs("NAF", h), OP.max)
        run("V", hs("OFFS", h)[1], hs("OT", h)[1], 0.07, [lambda: g.vector.transpose(hs("OT", h)[0], hs("OFFS", h)[0])])
        grp = []
        for v in range(2):
            for b in range(4):
                for k in range(2):
                    z = (2 * v + k) * 128
                    c = 128 * h + 32 * b + 16 * k
                    grp.append((R("M5", 128 * h + 4 * v + b, 128 * h + 128, 8), R("SV", z, z + 128), R("OT", c, c + 16), k == 0, k == 1))
        mms(*grp)
        cp(hs("MO", h), R("M5", 128 * h, 128 * h + 128))
        for p in range(16):
            act(IND("FL" if p % 2 else "FM", 0, EALL, "MO", 128 * h + 8 * p, 128 * h + 8 * p + 8), R("MV", 256 * w, 256 * w + 128), AF.Silu)

    def succeeded(w):
        act(IND("FL", 0, EALL, "ISU", 0, 16), R("MV", 1024, 1280), AF.Silu)
        act(full("FMB"), R("FM", 0, NOWN), AF.Copy)
        act(full("FLB"), R("FL", 0, NOWN), AF.Copy)

    def parity(w):
        ts(full("PC"), full("B0"), 0.0, OP.is_gt)
        run("V", rds(full("PC")), [("PR", 0, 1)], 0.07,
            [lambda: g.vector.tensor_reduce(T["PR"][:, 0:1], T["PC"][:, 0:16], axis=AxisListType.X, op=OP.add)])
        cp(full("PR16"), full("PR"))
        mms((R("F7", 64, 65), full("O16"), full("PR16"), True, True))
        cp(full("PINT"), R("F7", 64, 65))
        ts(full("PINT"), full("PINT"), 1, OP.bitwise_and)
        ts(R("MC", w + 1, w + 2), full("PINT"), -8.0, OP.mult, MAG + 8.0, OP.add)

    def front_c(w):
        for nm, k in (("FMB", 192), ("FLB", 128)):
            mms(*[(R("F6", k, k + 64), R("DGB", c * 128, c * 128 + 128), R(nm, c, 1024, 16), c == 0, c == 15) for c in range(16)])
        c = R("F6", 128, 192)
        ts(full("T3"), R("F6", 192, 256), 4.0 * w + 2.0, OP.is_gt)
        ts(full("T2"), c, 4.0 * w + 2.0, OP.is_gt)
        ts(full("NT"), c, 60.0, OP.is_ge)
        tt(full("XX"), full("WTL"), full("T3"), OP.max)
        tt(full("XX"), full("XX"), full("T2"), OP.max)
        tt(full("NE"), full("NE"), full("NT"), OP.max)
        tt(full("AV"), full("XX"), full("NE"), OP.is_gt)
        front_a(w + 1, 64)

    def numbers(w, h):
        x = R("XR%d" % (w % 2), 2048 * h, 2048 * h + 2048, 16)
        tt(hs("DX", h), IND("BT", 0, 4097, "BU", 8 * h, 8 * h + 8), x, OP.subtract)
        ts(hs("CL", h), hs("DX", h), -2.0, OP.max, 2.0, OP.min)
        tt(hs("NX", h), hs("CL", h), x, OP.add)
        cp(IND("YA", 0, EW, "ISU", 8 * h, 8 * h + 8), hs("NX", h))

    for w in range(WAVES):
        last = w == WAVES - 1
        for h in range(2):
            seeds(h, 0)
            seeds(h, 1)
            seeds_end(h)
        if not last:
            credit(w + 1)
        else:
            act(R("YF", 0, NOWN), R("E", 0, NOWN), AF.Identity, bias=-1.0)
            act(full("YT"), R("E", 0, NOWN), AF.Identity, bias=4095.0, scale=-5000.0)
            tt(R("YF", 0, NOWN), R("YF", 0, NOWN), full("YT"), OP.max)
        for t in range(3):
            for h in range(2):
                near(w, t, h, 0)
                near(w, t, h, 1)
                seg1(w, t, h)
                seg2(w, t, h)
                if t == 0 and not last:
                    marks(w, h)
                seg3(w, t, h)
            if t == 0:
                idxs(w)
                if not last:
                    succeeded(w)
                    parity(w)
                    front_c(w)
            if t == 2:
                if not last:
                    ghosts(w + 1)
                else:
                    store("Y", "oF", T.yf[:], R("YF", 0, NOWN))
                numbers(w, 0)
                numbers(w, 1)
                if not last:
                    front_b(w + 1)
    store("Y", "oA", T.ya[:], R("YA", 0, NOWN))
    issue()

    for s in "VSPG":
        g.wait_ge(T.sem["c" + s], cnt[s])
    for x in LOADS:
        g.wait_ge(T.sem["d_" + x], 16)
    ne = len(topo.engines(core, nxt))
    for w in range(WAVES):
        g.wait_ge(T.sem["gArr%d" % w], ne)
        g.wait_ge(T.sem["gLoc%d" % w], ne)
    for s in ("bArr", "nArr", "bLoc", "nLoc"):
        g.wait_ge(T.sem[s], len(topo.engines(core, prv)))
    g.wait_ge(T.sem["crLoc"], WAVES - 1)
